import numpy as np
import ml_dtypes


def mxq(x, axis, fmt="e4m3"):
    dtype, down = {"e4m3": (ml_dtypes.float8_e4m3fn, 7), "e5m2": (ml_dtypes.float8_e5m2, 14)}[fmt]
    v = np.moveaxis(np.asarray(x, np.float32).astype(ml_dtypes.bfloat16).astype(np.float64), axis, -1)
    blocks = v.reshape(v.shape[:-1] + (-1, 32))
    amax = np.abs(blocks).max(-1, keepdims=True)
    byte = np.maximum(np.where(amax > 0, np.frexp(amax)[1] - 1 + 127, 0) - down, 1)
    scale = np.exp2(byte - 127.0)
    codes = (blocks / scale).astype(np.float32).astype(dtype).astype(np.float64)
    return np.moveaxis((codes * scale).reshape(v.shape), -1, axis)


WIDE = False


def mx_kscale(k):
    if not WIDE:
        return np.ones(k)
    levels = np.array([10, -10, 5, -5, 0])
    if k % 512:
        return np.exp2(np.random.permutation(np.resize(levels, k // 32))).repeat(32)
    a = np.empty((k // 512, 16))
    for p in range(k // 512):
        a[p, :8] = np.random.permutation(np.resize(levels, 8))
        for g in range(8):
            far = levels[np.abs(levels - a[p, g]) >= 10]
            a[p, g + 8] = far[np.random.randint(len(far))]
    return np.exp2(a.ravel()).repeat(32)


def f64(x):
    return np.asarray(x).astype(np.float64)


def striped(idx):
    return np.tile(idx.reshape(-1, 16).T, (8, 1)).astype(np.uint16)


def unstriped(offs):
    return offs[:16].T.reshape(-1).astype(np.int64)


K, T, E, C, N = 512, 4096, 12, 128, 384


def by_expert(wq, xq):
    return np.concatenate([wq[e].T @ xq[:, e * C:(e + 1) * C] for e in range(E)], axis=1)


def setup_inputs():
    n = np.random.standard_normal
    s = mx_kscale(K)[:, None]
    return {
        "xT": (n((K, T)) * s).astype(np.float32),
        "w": (n((E, K, N)) / np.sqrt(K) / s[None]).astype(np.float32),
        "b": (0.3 * n((N, E))).astype(np.float32),
        "gate": np.tile(np.random.uniform(0.2, 1.0, E * C), (N, 1)).astype(np.float32),
        "offs": striped(np.random.permutation(T)[:E * C]),
    }


def reference(xT, w, b, gate, offs):
    idx = unstriped(offs)
    xq = mxq(f64(xT)[:, idx], 0, "e4m3")
    y = by_expert(mxq(f64(w), 1, "e4m3"), xq)
    y = y + np.repeat(f64(b), C, axis=1)
    out = np.zeros((N, T))
    out[:, idx] = f64(gate) * y
    return out

@@ -1,0 +1,188 @@
+from contextlib import ExitStack
+
+import concourse.mybir as mybir
+
+K, T, E, C, N = 512, 4096, 12, 128, 384
+SLOTS = E * C
+FLOPS = 2 * K * N * SLOTS
+
+F32 = mybir.dt.float32
+BF16 = mybir.dt.bfloat16
+U32 = mybir.dt.uint32
+U16 = mybir.dt.uint16
+U8 = mybir.dt.uint8
+FP8X4 = mybir.dt.float8_e4m3fn_x4
+MULT = mybir.AluOpType.mult
+IDENT = mybir.ActivationFunctionType.Identity
+
+P = 128
+PACK = 4
+BLOCKS = N // P
+GROUP = 512
+GROUPS = SLOTS // GROUP
+PER_GROUP = GROUP // C
+COLS = GROUP // 16
+
+
+def tile_routed_moe_kernel(tc, xT, w, b, gate, offs, out):
+    nc = tc.nc
+    x_planes = xT.rearrange("(p t) n -> p t n", t=PACK)
+    gate_rows = gate.rearrange("(m p) j -> p m j", p=P)
+
+    with ExitStack() as ctx:
+        keep = ctx.enter_context(tc.tile_pool(name="keep", bufs=1))
+        big = ctx.enter_context(tc.tile_pool(name="big", bufs=4))
+        wpool = ctx.enter_context(tc.tile_pool(name="wpool", bufs=2))
+        ypool = ctx.enter_context(tc.tile_pool(name="ypool", bufs=4))
+        psum = ctx.enter_context(tc.psum_pool(name="psum", bufs=8))
+
+        offsets = keep.tile([P, SLOTS // 16], U16, name="offsets")
+        nc.sync.dma_start(offsets[:], offs)
+
+        warm = keep.tile([P, 1], F32, name="warm")
+        nc.vector.memset(warm[:], 0.0)
+        nc.scalar.activation(warm[:], warm[:], IDENT)
+
+        wins = [keep.tile([P, T], F32, name=f"win{m}") for m in range(BLOCKS)]
+        nc.vector.memset(wins[0][:], 0.0)
+        nc.vector.memset(wins[1][:], 0.0)
+        nc.gpsimd.memset(wins[2][:], 0.0)
+
+        planes = []
+        for t in range(PACK):
+            plane = big.tile([P, T], F32, name="big")
+            nc.sync.dma_start(plane[:], x_planes[:, t, :])
+            planes.append(plane)
+
+        bias = keep.tile([P, BLOCKS, E], F32, name="bias")
+        nc.sync.dma_start(bias[:], b.rearrange("(m p) e -> p m e", p=P))
+
+        raws = {}
+        gates = {}
+
+        def load_w(e):
+            if e % 2 == 0:
+                raws[e // 2] = big.tile([P, 2, PACK, N], F32, name="big")
+            nc.sync.dma_start(raws[e // 2][:, e % 2, :, :], w[e].rearrange("(p t) n -> p t n", t=PACK))
+
+        def load_gate(g, m):
+            gates[g, m] = keep.tile([P, GROUP], F32, name=f"gate{g}_{m}")
+            nc.sync.dma_start(gates[g, m][:], gate_rows[:, m, g * GROUP : (g + 1) * GROUP])
+
+        for g in range(GROUPS):
+            for e in range(PER_GROUP * g, PER_GROUP * (g + 1)):
+                load_w(e)
+            for m in range(BLOCKS):
+                load_gate(g, m)
+
+        pairs = [keep.tile([P, 2, SLOTS], F32, name=f"pair{u}") for u in range(2)]
+        mixed_x = [keep.tile([P, GROUP, PACK], BF16, name=f"mixed{g}", align_bytes=64) for g in range(GROUPS)]
+        x_codes = [keep.tile([P, GROUP], U32, name=f"xcodes{g}", align_bytes=64) for g in range(GROUPS)]
+        x_scales = [keep.tile([P, GROUP], U8, name=f"xscales{g}", align_bytes=64) for g in range(GROUPS)]
+
+        def interleave_pair(u, g):
+            nc.scalar.copy(
+                mixed_x[g][:, :, 2 * u : 2 * u + 2],
+                pairs[u][:, :, g * GROUP : (g + 1) * GROUP].rearrange("p t n -> p n t"),
+            )
+
+        def gather_last(g):
+            nc.vector.tensor_copy(
+                pairs[1][:, 1, g * GROUP : (g + 1) * GROUP],
+                planes[3][:].indirect(offsets[:, g * COLS : (g + 1) * COLS]),
+            )
+
+        def quantise_x(g):
+            interleave_pair(1, g)
+            nc.vector.quantize_mx(
+                out=x_codes[g][:].bitcast(FP8X4),
+                scales=x_scales[g][:],
+                in_=mixed_x[g][:].rearrange("p n t -> p (n t)"),
+            )
+
+        for t in range(PACK - 1):
+            nc.vector.tensor_copy(pairs[t // 2][:, t % 2, :], planes[t][:].indirect(offsets[:]))
+        for g in range(GROUPS):
+            interleave_pair(0, g)
+
+        mixed_w, w_codes, w_scales = {}, {}, {}
+        for g in range(GROUPS):
+            w_codes[g] = keep.tile([P, PER_GROUP * N], U32, name=f"wcodes{g}", align_bytes=64)
+            w_scales[g] = keep.tile([P, PER_GROUP * N], U8, name=f"wscales{g}", align_bytes=64)
+
+        def interleave_w(e, engine, lo=0, hi=N):
+            g, i = divmod(e, PER_GROUP)
+            if g not in mixed_w:
+                mixed_w[g] = wpool.tile([P, PER_GROUP * N, PACK], BF16, name="wmixed", align_bytes=64)
+            dst = mixed_w[g][:, i * N + lo : i * N + hi, :]
+            src = raws[e // 2][:, e % 2, :, lo:hi].rearrange("p t n -> p n t")
+            if engine == "v":
+                nc.vector.tensor_copy(dst, src)
+            else:
+                nc.scalar.copy(dst, src)
+
+        def quantise_w(g, lo, hi):
+            nc.vector.quantize_mx(
+                out=w_codes[g][:, lo:hi].bitcast(FP8X4),
+                scales=w_scales[g][:, lo:hi],
+                in_=mixed_w[g][:].rearrange("p n t -> p (n t)")[:, lo * PACK : hi * PACK],
+            )
+
+        def multiply(g, m):
+            acc = psum.tile([P, GROUP], F32, name="acc")
+            y = ypool.tile([P, GROUP], F32, name="y")
+            for i in range(PER_GROUP):
+                e = g * PER_GROUP + i
+                cols = slice(i * N + m * P, i * N + (m + 1) * P)
+                here = slice(i * C, (i + 1) * C)
+                nc.tensor.matmul_mx(
+                    out=acc[:, here],
+                    lhsT=w_codes[g][:, cols].bitcast(FP8X4),
+                    lhsT_scale=w_scales[g][:, cols],
+                    rhs=x_codes[g][:, here].bitcast(FP8X4),
+                    rhs_scale=x_scales[g][:, here],
+                    start=True,
+                    stop=True,
+                )
+                nc.scalar.activation(y[:, here], acc[:, here], IDENT, bias=bias[:, m, e : e + 1])
+            nc.vector.tensor_tensor(
+                wins[m][:].indirect(offsets[:, g * COLS : (g + 1) * COLS]), y[:], gates[g, m][:], MULT
+            )
+
+        def store(m):
+            nc.sync.dma_start(out[m * P : (m + 1) * P, :], wins[m][:])
+
+        gather_last(0)
+        quantise_x(0)
+        for e, engine in enumerate("svs"):
+            interleave_w(e, engine)
+            quantise_w(0, e * N, e * N + 256)
+            quantise_w(0, e * N + 256, e * N + N)
+        interleave_w(3, "v", 0, P)
+        quantise_w(0, 3 * N, 3 * N + P)
+        multiply(0, 0)
+        gather_last(1)
+        gather_last(2)
+        interleave_w(3, "s", P, N)
+        quantise_w(0, 3 * N + P, 4 * N)
+        multiply(0, 1)
+        multiply(0, 2)
+        quantise_x(1)
+        for e, engine in enumerate("sssv"):
+            interleave_w(4 + e, engine)
+        quantise_w(1, 0, 1024)
+        quantise_w(1, 1024, 1536)
+        multiply(1, 0)
+        multiply(1, 1)
+        quantise_x(2)
+        for e, engine in enumerate("sssv"):
+            interleave_w(8 + e, engine)
+        quantise_w(2, 0, 1024)
+        quantise_w(2, 1024, 1536)
+        multiply(2, 0)
+        store(0)
+        multiply(2, 1)
+        store(1)
+        multiply(1, 2)
+        multiply(2, 2)
+        store(2)

@@ -21,7 +21,8 @@ BLOCKS = N // P
 GROUP = 512
 GROUPS = SLOTS // GROUP
 PER_GROUP = GROUP // C
-COLS = GROUP // 16
+
+CHUNKS = [(0, 0, 2048, 1024), (0, 2048, 2048, 1024), (1, 0, 2048, 1024), (1, 2048, 1024, 384), (1, 3072, 1024, 384)]
 
 
 def tile_routed_moe_kernel(tc, xT, w, b, gate, offs, out):
@@ -31,158 +32,176 @@ def tile_routed_moe_kernel(tc, xT, w, b, gate, offs, out):
 
     with ExitStack() as ctx:
         keep = ctx.enter_context(tc.tile_pool(name="keep", bufs=1))
-        big = ctx.enter_context(tc.tile_pool(name="big", bufs=4))
+        rawpool = ctx.enter_context(tc.tile_pool(name="rawpool", bufs=3))
         wpool = ctx.enter_context(tc.tile_pool(name="wpool", bufs=2))
         ypool = ctx.enter_context(tc.tile_pool(name="ypool", bufs=4))
         psum = ctx.enter_context(tc.psum_pool(name="psum", bufs=8))
 
         offsets = keep.tile([P, SLOTS // 16], U16, name="offsets")
-        nc.sync.dma_start(offsets[:], offs)
+
+        def listed(g0, g1):
+            return offsets[:, g0 * GROUP // 16 : g1 * GROUP // 16]
+
+        chunks = []
+        for u, t0, count, share in CHUNKS:
+            raw = rawpool.tile([P, 2, count], F32, name="raw")
+            nc.sync.dma_start(raw[:], x_planes[:, 2 * u : 2 * u + 2, t0 : t0 + count])
+            chunks.append(raw)
+            if len(chunks) == 1:
+                nc.sync.dma_start(offsets[:], offs)
+
+        bias = keep.tile([P, BLOCKS, E], F32, name="bias")
+        raws, gates = {}, {}
+
+        def load_w(e):
+            if e % 2 == 0:
+                raws[e // 2] = rawpool.tile([P, 2, PACK, N], F32, name="raw")
+            nc.sync.dma_start(raws[e // 2][:, e % 2, :, :], w[e].rearrange("(p t) n -> p t n", t=PACK))
+
+        def load_gate(m, g0, g1):
+            tile = keep.tile([P, (g1 - g0) * GROUP], F32, name=f"gate{g0}_{m}")
+            nc.sync.dma_start(tile[:], gate_rows[:, m, g0 * GROUP : g1 * GROUP])
+            for g in range(g0, g1):
+                gates[g, m] = (tile, (g - g0) * GROUP)
+
+        load_w(0)
+        nc.sync.dma_start(bias[:], b.rearrange("(m p) e -> p m e", p=P))
+        for e in (1, 2, 3):
+            load_w(e)
+        for m in range(BLOCKS):
+            load_gate(m, 0, 1)
+        for e in range(4, 8):
+            load_w(e)
+        load_gate(0, 1, 3)
+        load_gate(1, 1, 3)
+        for e in range(8, 12):
+            load_w(e)
+        load_gate(2, 1, 3)
 
         warm = keep.tile([P, 1], F32, name="warm")
         nc.vector.memset(warm[:], 0.0)
         nc.scalar.activation(warm[:], warm[:], IDENT)
-
         wins = [keep.tile([P, T], F32, name=f"win{m}") for m in range(BLOCKS)]
         nc.vector.memset(wins[0][:], 0.0)
-        nc.vector.memset(wins[1][:], 0.0)
+        nc.gpsimd.memset(wins[1][:], 0.0)
         nc.gpsimd.memset(wins[2][:], 0.0)
 
-        planes = []
-        for t in range(PACK):
-            plane = big.tile([P, T], F32, name="big")
-            nc.sync.dma_start(plane[:], x_planes[:, t, :])
-            planes.append(plane)
+        tokens = [keep.tile([P, T, 2], BF16, name=f"tokens{u}") for u in range(2)]
+        mixed_x = keep.tile([P, SLOTS, PACK], BF16, name="mixedx", align_bytes=64)
+        mixed_words = mixed_x[:].rearrange("p n t -> p (n t)").bitcast(U32).rearrange("p (n u) -> p n u", u=2)
+        x_codes = keep.tile([P, SLOTS], U32, name="xcodes", align_bytes=64)
+        x_scales = keep.tile([P, SLOTS], U8, name="xscales", align_bytes=64)
 
-        bias = keep.tile([P, BLOCKS, E], F32, name="bias")
-        nc.sync.dma_start(bias[:], b.rearrange("(m p) e -> p m e", p=P))
+        def cast_chunk(i):
+            u, t0, count, share = CHUNKS[i]
+            for engine_copy, lo, hi in ((nc.scalar.copy, 0, share), (nc.vector.tensor_copy, share, count)):
+                engine_copy(
+                    tokens[u][:, t0 + lo : t0 + hi, :], chunks[i][:, :, lo:hi].rearrange("p u n -> p n u")
+                )
 
-        raws = {}
-        gates = {}
-
-        def load_w(e):
-            if e % 2 == 0:
-                raws[e // 2] = big.tile([P, 2, PACK, N], F32, name="big")
-            nc.sync.dma_start(raws[e // 2][:, e % 2, :, :], w[e].rearrange("(p t) n -> p t n", t=PACK))
-
-        def load_gate(g, m):
-            gates[g, m] = keep.tile([P, GROUP], F32, name=f"gate{g}_{m}")
-            nc.sync.dma_start(gates[g, m][:], gate_rows[:, m, g * GROUP : (g + 1) * GROUP])
-
-        for g in range(GROUPS):
-            for e in range(PER_GROUP * g, PER_GROUP * (g + 1)):
-                load_w(e)
-            for m in range(BLOCKS):
-                load_gate(g, m)
-
-        pairs = [keep.tile([P, 2, SLOTS], F32, name=f"pair{u}") for u in range(2)]
-        mixed_x = [keep.tile([P, GROUP, PACK], BF16, name=f"mixed{g}", align_bytes=64) for g in range(GROUPS)]
-        x_codes = [keep.tile([P, GROUP], U32, name=f"xcodes{g}", align_bytes=64) for g in range(GROUPS)]
-        x_scales = [keep.tile([P, GROUP], U8, name=f"xscales{g}", align_bytes=64) for g in range(GROUPS)]
-
-        def interleave_pair(u, g):
-            nc.scalar.copy(
-                mixed_x[g][:, :, 2 * u : 2 * u + 2],
-                pairs[u][:, :, g * GROUP : (g + 1) * GROUP].rearrange("p t n -> p n t"),
-            )
-
-        def gather_last(g):
+        def gather_x(u, g0, g1):
             nc.vector.tensor_copy(
-                pairs[1][:, 1, g * GROUP : (g + 1) * GROUP],
-                planes[3][:].indirect(offsets[:, g * COLS : (g + 1) * COLS]),
+                mixed_words[:, g0 * GROUP : g1 * GROUP, u],
+                tokens[u][:].rearrange("p n u -> p (n u)").bitcast(U32).indirect(listed(g0, g1)),
             )
 
-        def quantise_x(g):
-            interleave_pair(1, g)
+        def quantise_x(g0, g1):
+            here = slice(g0 * GROUP, g1 * GROUP)
             nc.vector.quantize_mx(
-                out=x_codes[g][:].bitcast(FP8X4),
-                scales=x_scales[g][:],
-                in_=mixed_x[g][:].rearrange("p n t -> p (n t)"),
+                out=x_codes[:, here].bitcast(FP8X4),
+                scales=x_scales[:, here],
+                in_=mixed_x[:, here, :].rearrange("p n t -> p (n t)"),
             )
 
-        for t in range(PACK - 1):
-            nc.vector.tensor_copy(pairs[t // 2][:, t % 2, :], planes[t][:].indirect(offsets[:]))
-        for g in range(GROUPS):
-            interleave_pair(0, g)
+        mixed_w = {}
+        w_codes = [keep.tile([P, PER_GROUP * N], U32, name=f"wcodes{g}", align_bytes=64) for g in range(GROUPS)]
+        w_scales = [keep.tile([P, PER_GROUP * N], U8, name=f"wscales{g}", align_bytes=64) for g in range(GROUPS)]
 
-        mixed_w, w_codes, w_scales = {}, {}, {}
-        for g in range(GROUPS):
-            w_codes[g] = keep.tile([P, PER_GROUP * N], U32, name=f"wcodes{g}", align_bytes=64)
-            w_scales[g] = keep.tile([P, PER_GROUP * N], U8, name=f"wscales{g}", align_bytes=64)
-
-        def interleave_w(e, engine, lo=0, hi=N):
+        def interleave_w(e, copy, lo=0, hi=N):
             g, i = divmod(e, PER_GROUP)
             if g not in mixed_w:
                 mixed_w[g] = wpool.tile([P, PER_GROUP * N, PACK], BF16, name="wmixed", align_bytes=64)
-            dst = mixed_w[g][:, i * N + lo : i * N + hi, :]
-            src = raws[e // 2][:, e % 2, :, lo:hi].rearrange("p t n -> p n t")
-            if engine == "v":
-                nc.vector.tensor_copy(dst, src)
-            else:
-                nc.scalar.copy(dst, src)
-
-        def quantise_w(g, lo, hi):
-            nc.vector.quantize_mx(
-                out=w_codes[g][:, lo:hi].bitcast(FP8X4),
-                scales=w_scales[g][:, lo:hi],
-                in_=mixed_w[g][:].rearrange("p n t -> p (n t)")[:, lo * PACK : hi * PACK],
+            copy(
+                mixed_w[g][:, i * N + lo : i * N + hi, :].rearrange("p (c i) t -> p c t i", i=4),
+                raws[e // 2][:, e % 2, :, lo:hi].rearrange("p t (c i) -> p c t i", i=4),
             )
 
-        def multiply(g, m):
-            acc = psum.tile([P, GROUP], F32, name="acc")
-            y = ypool.tile([P, GROUP], F32, name="y")
-            for i in range(PER_GROUP):
-                e = g * PER_GROUP + i
-                cols = slice(i * N + m * P, i * N + (m + 1) * P)
-                here = slice(i * C, (i + 1) * C)
-                nc.tensor.matmul_mx(
-                    out=acc[:, here],
-                    lhsT=w_codes[g][:, cols].bitcast(FP8X4),
-                    lhsT_scale=w_scales[g][:, cols],
-                    rhs=x_codes[g][:, here].bitcast(FP8X4),
-                    rhs_scale=x_scales[g][:, here],
-                    start=True,
-                    stop=True,
+        def quantise_w(g, *edges):
+            for lo, hi in zip(edges, edges[1:]):
+                nc.vector.quantize_mx(
+                    out=w_codes[g][:, lo:hi].bitcast(FP8X4),
+                    scales=w_scales[g][:, lo:hi],
+                    in_=mixed_w[g][:].rearrange("p n t -> p (n t)")[:, lo * PACK : hi * PACK],
                 )
-                nc.scalar.activation(y[:, here], acc[:, here], IDENT, bias=bias[:, m, e : e + 1])
+
+        def multiply(m, g0, g1):
+            y = ypool.tile([P, (g1 - g0) * GROUP], F32, name="y" if g1 == g0 + 1 else "ylong", bufs=4 if g1 == g0 + 1 else 1)
+            for g in range(g0, g1):
+                accs = []
+                for i in range(PER_GROUP):
+                    if i == 0 or i == (3 if (g, m) == (0, 0) else 2):
+                        acc = psum.tile([P, GROUP], F32, name="acc")
+                    accs.append(acc)
+                    cols = slice(i * N + m * P, i * N + (m + 1) * P)
+                    slots = slice((g * PER_GROUP + i) * C, (g * PER_GROUP + i + 1) * C)
+                    nc.tensor.matmul_mx(
+                        out=acc[:, i * C : (i + 1) * C],
+                        lhsT=w_codes[g][:, cols].bitcast(FP8X4),
+                        lhsT_scale=w_scales[g][:, cols],
+                        rhs=x_codes[:, slots].bitcast(FP8X4),
+                        rhs_scale=x_scales[:, slots],
+                        start=True,
+                        stop=True,
+                    )
+                for i in range(PER_GROUP):
+                    e = g * PER_GROUP + i
+                    at = (g - g0) * GROUP + i * C
+                    nc.scalar.activation(
+                        y[:, at : at + C], accs[i][:, i * C : (i + 1) * C], IDENT, bias=bias[:, m, e : e + 1]
+                    )
+            gate_tile, at = gates[g0, m]
             nc.vector.tensor_tensor(
-                wins[m][:].indirect(offsets[:, g * COLS : (g + 1) * COLS]), y[:], gates[g, m][:], MULT
+                wins[m][:].indirect(listed(g0, g1)), y[:], gate_tile[:, at : at + (g1 - g0) * GROUP], MULT
             )
 
         def store(m):
             nc.sync.dma_start(out[m * P : (m + 1) * P, :], wins[m][:])
 
-        gather_last(0)
-        quantise_x(0)
-        for e, engine in enumerate("svs"):
-            interleave_w(e, engine)
-            quantise_w(0, e * N, e * N + 256)
-            quantise_w(0, e * N + 256, e * N + N)
-        interleave_w(3, "v", 0, P)
-        quantise_w(0, 3 * N, 3 * N + P)
-        multiply(0, 0)
-        gather_last(1)
-        gather_last(2)
-        interleave_w(3, "s", P, N)
-        quantise_w(0, 3 * N + P, 4 * N)
-        multiply(0, 1)
-        multiply(0, 2)
-        quantise_x(1)
-        for e, engine in enumerate("sssv"):
-            interleave_w(4 + e, engine)
-        quantise_w(1, 0, 1024)
-        quantise_w(1, 1024, 1536)
-        multiply(1, 0)
-        multiply(1, 1)
-        quantise_x(2)
-        for e, engine in enumerate("sssv"):
-            interleave_w(8 + e, engine)
-        quantise_w(2, 0, 1024)
-        quantise_w(2, 1024, 1536)
-        multiply(2, 0)
+        v, s = nc.vector.tensor_copy, nc.scalar.copy
+        cast_chunk(0)
+        cast_chunk(1)
+        gather_x(0, 0, 3)
+        for i in (2, 3, 4):
+            cast_chunk(i)
+        gather_x(1, 0, 1)
+        quantise_x(0, 1)
+        interleave_w(0, s)
+        interleave_w(1, s)
+        quantise_w(0, 0, 512, 768)
+        interleave_w(2, s)
+        quantise_w(0, 768, 1024, 1152)
+        interleave_w(3, v, 0, P)
+        quantise_w(0, 1152, 1280)
+        multiply(0, 0, 1)
+        gather_x(1, 1, 3)
+        quantise_x(1, 3)
+        interleave_w(3, v, P, N)
+        quantise_w(0, 1280, 1536)
+        multiply(1, 0, 1)
+        interleave_w(4, s)
+        interleave_w(5, s)
+        interleave_w(6, s)
+        interleave_w(7, v)
+        quantise_w(1, 0, 1024, 1536)
+        multiply(2, 0, 1)
+        multiply(0, 1, 2)
+        for e in range(8, 12):
+            interleave_w(e, s)
+        quantise_w(2, 0, 1024, 1536)
+        multiply(1, 1, 2)
+        multiply(0, 2, 3)
         store(0)
-        multiply(2, 1)
+        multiply(1, 2, 3)
         store(1)
-        multiply(1, 2)
-        multiply(2, 2)
+        multiply(2, 1, 3)
         store(2)

@@ -22,7 +22,7 @@ GROUP = 512
 GROUPS = SLOTS // GROUP
 PER_GROUP = GROUP // C
 
-CHUNKS = [(0, 0, 2048, 1024), (0, 2048, 2048, 1024), (1, 0, 2048, 1024), (1, 2048, 1024, 384), (1, 3072, 1024, 384)]
+CHUNKS = [(0, 0, 2048, 1024), (0, 2048, 2048, 1024), (1, 0, 2048, 1024), (1, 2048, 1536, 576), (1, 3584, 512, 0)]
 
 
 def tile_routed_moe_kernel(tc, xT, w, b, gate, offs, out):
@@ -64,18 +64,19 @@ def tile_routed_moe_kernel(tc, xT, w, b, gate, offs, out):
             for g in range(g0, g1):
                 gates[g, m] = (tile, (g - g0) * GROUP)
 
-        load_w(0)
-        nc.sync.dma_start(bias[:], b.rearrange("(m p) e -> p m e", p=P))
-        for e in (1, 2, 3):
+        for e in range(4):
             load_w(e)
-        for m in range(BLOCKS):
-            load_gate(m, 0, 1)
-        for e in range(4, 8):
+        nc.sync.dma_start(bias[:], b.rearrange("(m p) e -> p m e", p=P))
+        load_gate(0, 0, 1)
+        load_gate(1, 0, 1)
+        load_w(4)
+        load_w(5)
+        load_gate(2, 0, 1)
+        for e in range(6, 11):
             load_w(e)
         load_gate(0, 1, 3)
+        load_w(11)
         load_gate(1, 1, 3)
-        for e in range(8, 12):
-            load_w(e)
         load_gate(2, 1, 3)
 
         warm = keep.tile([P, 1], F32, name="warm")
@@ -95,7 +96,8 @@ def tile_routed_moe_kernel(tc, xT, w, b, gate, offs, out):
         def cast_chunk(i):
             u, t0, count, share = CHUNKS[i]
             for engine_copy, lo, hi in ((nc.scalar.copy, 0, share), (nc.vector.tensor_copy, share, count)):
-                engine_copy(
+                if hi > lo:
+                  engine_copy(
                     tokens[u][:, t0 + lo : t0 + hi, :], chunks[i][:, :, lo:hi].rearrange("p u n -> p n u")
                 )
 
@@ -139,7 +141,7 @@ def tile_routed_moe_kernel(tc, xT, w, b, gate, offs, out):
             for g in range(g0, g1):
                 accs = []
                 for i in range(PER_GROUP):
-                    if i == 0 or i == (3 if (g, m) == (0, 0) else 2):
+                    if i in ((0, 2, 3) if m == 0 else (0, 2)):
                         acc = psum.tile([P, GROUP], F32, name="acc")
                     accs.append(acc)
                     cols = slice(i * N + m * P, i * N + (m + 1) * P)
@@ -180,26 +182,32 @@ def tile_routed_moe_kernel(tc, xT, w, b, gate, offs, out):
         quantise_w(0, 0, 512, 768)
         interleave_w(2, s)
         quantise_w(0, 768, 1024, 1152)
-        interleave_w(3, v, 0, P)
+        interleave_w(3, s, 0, P)
         quantise_w(0, 1152, 1280)
+        interleave_w(3, v, P, N)
+        quantise_w(0, 1280, 1536)
         multiply(0, 0, 1)
         gather_x(1, 1, 3)
         quantise_x(1, 3)
-        interleave_w(3, v, P, N)
-        quantise_w(0, 1280, 1536)
         multiply(1, 0, 1)
         interleave_w(4, s)
         interleave_w(5, s)
         interleave_w(6, s)
-        interleave_w(7, v)
-        quantise_w(1, 0, 1024, 1536)
+        interleave_w(7, s, 0, 192)
+        interleave_w(7, v, 192, N)
+        quantise_w(1, 0, 1024, 1280)
         multiply(2, 0, 1)
         multiply(0, 1, 2)
-        for e in range(8, 12):
-            interleave_w(e, s)
-        quantise_w(2, 0, 1024, 1536)
+        quantise_w(1, 1280, 1536)
+        interleave_w(8, s)
+        interleave_w(9, s, 0, 192)
+        interleave_w(9, v, 192, N)
+        interleave_w(10, s)
+        interleave_w(11, s)
+        quantise_w(2, 0, 1024, 1280)
         multiply(1, 1, 2)
         multiply(0, 2, 3)
+        quantise_w(2, 1280, 1536)
         store(0)
         multiply(1, 2, 3)
         store(1)

from contextlib import ExitStack

import concourse.mybir as mybir

K, T, E, C, N = 512, 4096, 12, 128, 384
SLOTS = E * C
FLOPS = 2 * K * N * SLOTS

F32 = mybir.dt.float32
BF16 = mybir.dt.bfloat16
U32 = mybir.dt.uint32
U16 = mybir.dt.uint16
U8 = mybir.dt.uint8
FP8X4 = mybir.dt.float8_e4m3fn_x4
MULT = mybir.AluOpType.mult
IDENT = mybir.ActivationFunctionType.Identity

P = 128
PACK = 4
BLOCKS = N // P
GROUP = 512
GROUPS = SLOTS // GROUP
PER_GROUP = GROUP // C

CHUNKS = [(0, 0, 2048, 1024), (0, 2048, 2048, 1024), (1, 0, 2048, 1024), (1, 2048, 1536, 576), (1, 3584, 512, 0)]


def tile_routed_moe_kernel(tc, xT, w, b, gate, offs, out):
    nc = tc.nc
    x_planes = xT.rearrange("(p t) n -> p t n", t=PACK)
    gate_rows = gate.rearrange("(m p) j -> p m j", p=P)

    with ExitStack() as ctx:
        keep = ctx.enter_context(tc.tile_pool(name="keep", bufs=1))
        rawpool = ctx.enter_context(tc.tile_pool(name="rawpool", bufs=3))
        wpool = ctx.enter_context(tc.tile_pool(name="wpool", bufs=2))
        ypool = ctx.enter_context(tc.tile_pool(name="ypool", bufs=4))
        psum = ctx.enter_context(tc.psum_pool(name="psum", bufs=8))

        offsets = keep.tile([P, SLOTS // 16], U16, name="offsets")

        def listed(g0, g1):
            return offsets[:, g0 * GROUP // 16 : g1 * GROUP // 16]

        chunks = []
        for u, t0, count, share in CHUNKS:
            raw = rawpool.tile([P, 2, count], F32, name="raw")
            nc.sync.dma_start(raw[:], x_planes[:, 2 * u : 2 * u + 2, t0 : t0 + count])
            chunks.append(raw)
            if len(chunks) == 1:
                nc.sync.dma_start(offsets[:], offs)

        bias = keep.tile([P, BLOCKS, E], F32, name="bias")
        raws, gates = {}, {}

        def load_w(e):
            if e % 2 == 0:
                raws[e // 2] = rawpool.tile([P, 2, PACK, N], F32, name="raw")
            nc.sync.dma_start(raws[e // 2][:, e % 2, :, :], w[e].rearrange("(p t) n -> p t n", t=PACK))

        def load_gate(m, g0, g1):
            tile = keep.tile([P, (g1 - g0) * GROUP], F32, name=f"gate{g0}_{m}")
            nc.sync.dma_start(tile[:], gate_rows[:, m, g0 * GROUP : g1 * GROUP])
            for g in range(g0, g1):
                gates[g, m] = (tile, (g - g0) * GROUP)

        for e in range(4):
            load_w(e)
        nc.sync.dma_start(bias[:], b.rearrange("(m p) e -> p m e", p=P))
        load_gate(0, 0, 1)
        load_gate(1, 0, 1)
        load_w(4)
        load_w(5)
        load_gate(2, 0, 1)
        for e in range(6, 11):
            load_w(e)
        load_gate(0, 1, 3)
        load_w(11)
        load_gate(1, 1, 3)
        load_gate(2, 1, 3)

        warm = keep.tile([P, 1], F32, name="warm")
        nc.vector.memset(warm[:], 0.0)
        nc.scalar.activation(warm[:], warm[:], IDENT)
        wins = [keep.tile([P, T], F32, name=f"win{m}") for m in range(BLOCKS)]
        nc.vector.memset(wins[0][:], 0.0)
        nc.gpsimd.memset(wins[1][:], 0.0)
        nc.gpsimd.memset(wins[2][:], 0.0)

        tokens = [keep.tile([P, T, 2], BF16, name=f"tokens{u}") for u in range(2)]
        mixed_x = keep.tile([P, SLOTS, PACK], BF16, name="mixedx", align_bytes=64)
        mixed_words = mixed_x[:].rearrange("p n t -> p (n t)").bitcast(U32).rearrange("p (n u) -> p n u", u=2)
        x_codes = keep.tile([P, SLOTS], U32, name="xcodes", align_bytes=64)
        x_scales = keep.tile([P, SLOTS], U8, name="xscales", align_bytes=64)

        def cast_chunk(i):
            u, t0, count, share = CHUNKS[i]
            for engine_copy, lo, hi in ((nc.scalar.copy, 0, share), (nc.vector.tensor_copy, share, count)):
                if hi > lo:
                  engine_copy(
                    tokens[u][:, t0 + lo : t0 + hi, :], chunks[i][:, :, lo:hi].rearrange("p u n -> p n u")
                )

        def gather_x(u, g0, g1):
            nc.vector.tensor_copy(
                mixed_words[:, g0 * GROUP : g1 * GROUP, u],
                tokens[u][:].rearrange("p n u -> p (n u)").bitcast(U32).indirect(listed(g0, g1)),
            )

        def quantise_x(g0, g1):
            here = slice(g0 * GROUP, g1 * GROUP)
            nc.vector.quantize_mx(
                out=x_codes[:, here].bitcast(FP8X4),
                scales=x_scales[:, here],
                in_=mixed_x[:, here, :].rearrange("p n t -> p (n t)"),
            )

        mixed_w = {}
        w_codes = [keep.tile([P, PER_GROUP * N], U32, name=f"wcodes{g}", align_bytes=64) for g in range(GROUPS)]
        w_scales = [keep.tile([P, PER_GROUP * N], U8, name=f"wscales{g}", align_bytes=64) for g in range(GROUPS)]

        def interleave_w(e, copy, lo=0, hi=N):
            g, i = divmod(e, PER_GROUP)
            if g not in mixed_w:
                mixed_w[g] = wpool.tile([P, PER_GROUP * N, PACK], BF16, name="wmixed", align_bytes=64)
            copy(
                mixed_w[g][:, i * N + lo : i * N + hi, :].rearrange("p (c i) t -> p c t i", i=4),
                raws[e // 2][:, e % 2, :, lo:hi].rearrange("p t (c i) -> p c t i", i=4),
            )

        def quantise_w(g, *edges):
            for lo, hi in zip(edges, edges[1:]):
                nc.vector.quantize_mx(
                    out=w_codes[g][:, lo:hi].bitcast(FP8X4),
                    scales=w_scales[g][:, lo:hi],
                    in_=mixed_w[g][:].rearrange("p n t -> p (n t)")[:, lo * PACK : hi * PACK],
                )

        def multiply(m, g0, g1):
            y = ypool.tile([P, (g1 - g0) * GROUP], F32, name="y" if g1 == g0 + 1 else "ylong", bufs=4 if g1 == g0 + 1 else 1)
            for g in range(g0, g1):
                accs = []
                for i in range(PER_GROUP):
                    if i in ((0, 2, 3) if m == 0 else (0, 2)):
                        acc = psum.tile([P, GROUP], F32, name="acc")
                    accs.append(acc)
                    cols = slice(i * N + m * P, i * N + (m + 1) * P)
                    slots = slice((g * PER_GROUP + i) * C, (g * PER_GROUP + i + 1) * C)
                    nc.tensor.matmul_mx(
                        out=acc[:, i * C : (i + 1) * C],
                        lhsT=w_codes[g][:, cols].bitcast(FP8X4),
                        lhsT_scale=w_scales[g][:, cols],
                        rhs=x_codes[:, slots].bitcast(FP8X4),
                        rhs_scale=x_scales[:, slots],
                        start=True,
                        stop=True,
                    )
                for i in range(PER_GROUP):
                    e = g * PER_GROUP + i
                    at = (g - g0) * GROUP + i * C
                    nc.scalar.activation(
                        y[:, at : at + C], accs[i][:, i * C : (i + 1) * C], IDENT, bias=bias[:, m, e : e + 1]
                    )
            gate_tile, at = gates[g0, m]
            nc.vector.tensor_tensor(
                wins[m][:].indirect(listed(g0, g1)), y[:], gate_tile[:, at : at + (g1 - g0) * GROUP], MULT
            )

        def store(m):
            nc.sync.dma_start(out[m * P : (m + 1) * P, :], wins[m][:])

        v, s = nc.vector.tensor_copy, nc.scalar.copy
        cast_chunk(0)
        cast_chunk(1)
        gather_x(0, 0, 3)
        for i in (2, 3, 4):
            cast_chunk(i)
        gather_x(1, 0, 1)
        quantise_x(0, 1)
        interleave_w(0, s)
        interleave_w(1, s)
        quantise_w(0, 0, 512, 768)
        interleave_w(2, s)
        quantise_w(0, 768, 1024, 1152)
        interleave_w(3, s, 0, P)
        quantise_w(0, 1152, 1280)
        interleave_w(3, v, P, N)
        quantise_w(0, 1280, 1536)
        multiply(0, 0, 1)
        gather_x(1, 1, 3)
        quantise_x(1, 3)
        multiply(1, 0, 1)
        interleave_w(4, s)
        interleave_w(5, s)
        interleave_w(6, s)
        interleave_w(7, s, 0, 192)
        interleave_w(7, v, 192, N)
        quantise_w(1, 0, 1024, 1280)
        multiply(2, 0, 1)
        multiply(0, 1, 2)
        quantise_w(1, 1280, 1536)
        interleave_w(8, s)
        interleave_w(9, s, 0, 192)
        interleave_w(9, v, 192, N)
        interleave_w(10, s)
        interleave_w(11, s)
        quantise_w(2, 0, 1024, 1280)
        multiply(1, 1, 2)
        multiply(0, 2, 3)
        quantise_w(2, 1280, 1536)
        store(0)
        multiply(1, 2, 3)
        store(1)
        multiply(2, 1, 3)
        store(2)
